import numpy as np, ml_dtypes
CORES = [3,5,19,21,35,37,51,53,67,69]
N = 10
import mx_ref
BF = ml_dtypes.bfloat16
def entries(a):
    return np.ascontiguousarray(a.T).reshape(-1)
def table(e):
    return np.ascontiguousarray(np.reshape(e, (-1, 16)).T).astype(np.int32)
def cols(t, e):
    v = np.concatenate([t.reshape(128, -1, 4), np.zeros((128, 1, 4), BF)], axis=1)
    return np.ascontiguousarray(v[:, e]).reshape(128, -1)
def f(rng, *shape):
    return mx_ref.flush((rng.standard_normal(shape, dtype=np.float32) * np.exp2(rng.integers(-2, 3, shape[:-1] + (1,)))).astype(BF))
def wide(rng, *shape, cols=0):
    v = rng.standard_normal(shape, dtype=np.float32) * np.exp2(rng.integers(-12, 13, shape)).astype(np.float32)
    if cols: v *= np.repeat(np.exp2(rng.integers(-cols, cols + 1, shape[:-2] + (1, shape[-1] // 4))) * (rng.random(shape[:-2] + (1, shape[-1] // 4)) > 0.0625), 4, axis=-1).astype(np.float32)
    return mx_ref.flush(v.astype(BF))
T, NA, S, CAPP = 512, 256, 512, 64
def lists(rng, most=0, inorder=False, big=None):
    c, m = [], []
    for r in range(N):
        n = np.zeros(N, int)
        n[rng.permutation(N)[:most]] = CAPP
        while n.sum() < S:
            q = rng.integers(0, N)
            if n[q] < CAPP: n[q] += 1
        used = np.concatenate([q * CAPP + rng.permutation(CAPP)[:n[q]] for q in range(N)])
        slots = np.full(N * CAPP, -1); slots[used] = rng.integers(0, T, S)
        o = np.sort(used) if inorder else rng.permutation(used)
        if big is not None:
            for i in range(S // 32):
                k = o[32 * i + rng.integers(0, 32)]; slots[k] = rng.choice(big[k // CAPP])
        c.append(table(slots)); m.append(table(o))
    return {"want": np.stack(c), "slot": np.stack(m)}
def setup_inputs(rng):
    return {"v": f(rng, N, 128, 4 * T), "a": f(rng, N, 128, 4 * NA), **lists(rng)}
def setup_inputs_full(rng):
    return {**setup_inputs(rng), **lists(rng, most=S // CAPP)}
def setup_inputs_sorted(rng):
    return {**setup_inputs(rng), **lists(rng, inorder=True)}
def setup_inputs_giant(rng):
    d = setup_inputs(rng); big = [rng.permutation(T)[:T // 32] for q in range(N)]
    x = d["v"].reshape(N, 128, T, 4)
    for q in range(N): x[q][:, big[q]] = (x[q][:, big[q]].astype(np.float32) * np.float32(2.0 ** 20)).astype(BF)
    d["v"] = x.reshape(N, 128, 4 * T)
    return {**d, **lists(rng, big=big)}
def setup_inputs_spread(rng):
    d = setup_inputs(rng); d["v"] = wide(rng, N, 128, 4 * T); d["a"] = wide(rng, N, 128, 4 * NA); return d
def check_inputs(d):
    b = []
    for r in range(N):
        c, m = entries(d["want"][r]), entries(d["slot"][r])
        if c.min() < -1 or c.max() >= T or (c >= 0).sum() != S: b.append("want")
        if m.min() < 0 or m.max() >= N * CAPP or len(set(m.tolist())) != S or (c[np.clip(m, 0, N * CAPP - 1)] < 0).any(): b.append("slot")
    return b
def ones(b):
    e = np.zeros((128, 128, 4), np.float32); e[np.arange(128), np.arange(128), b] = 1
    return e.reshape(128, 512).astype(BF)
def decode(q):
    return np.stack([mx_ref.matmul(mx_ref.quantize(ones(b)), q) for b in range(4)], axis=1).reshape(512, -1)
def reference(v, a, want, slot, own=None):
    h = np.zeros((N, 128, 2048), BF); y = np.zeros((N, 128, 4 * NA), np.float32)
    for r in range(N):
        c = entries(want[r])
        arrived = np.concatenate([decode(mx_ref.quantize(cols(v[q], c[q * CAPP:(q + 1) * CAPP]))) for q in range(N)], axis=1)
        H = arrived[:, entries(slot[r])].T
        h[r] = H.reshape(128, 4, 512).transpose(0, 2, 1).reshape(128, 2048).astype(BF)
    for r in range(N):
        t = h[r] if own is None else np.asarray(own["h"][r])
        for o in range(4):
            y[r][:, NA * o:NA * o + NA] = mx_ref.matmul(mx_ref.quantize(np.ascontiguousarray(t[:, 512 * o:512 * o + 512])), mx_ref.quantize(a[r]))
    return {"y": y, "h": h}

from concourse.bass import DstId, RemoteDMATransfer
from concourse.mybir import dt, AluOpType, ActivationFunctionType

BF, F32, I32, U16, CODE, U8 = "bfloat16", "float32", "int32", "uint16", "float8_e4m3fn_x4", "uint8"
SCRATCH = {
    "wl": ("sbuf", [128, 40], I32),
    "sw": ("sbuf", [128, 32], I32),
    "loff": ("sbuf", [128, 40], U16),
    "lown": ("sbuf", [128, 4], U16),
    "lst1": ("sbuf", [128, 16], U16),
    "lst2": ("sbuf", [128, 20], U16),
    "s1i": ("sbuf", [128, 32], I32),
    "s2i": ("sbuf", [128, 32], I32),
    "s3i": ("sbuf", [128, 32], I32),
    "sl": ("sbuf", [128, 32], U16),
    "vt": ("sbuf", [128, 2048], BF),
    "at": ("sbuf", [128, 1024], BF),
    "gt1": ("sbuf", [128, 1024], BF),
    "gt2": ("sbuf", [128, 1536], BF),
    "e1": ("sbuf", [128, 512], BF),
    "e2": ("sbuf", [128, 4], F32),
    "e3": ("sbuf", [128, 128], F32),
    "idt": ("sbuf", [128, 2048], BF),
    "idn": ("sbuf", [128, 128], F32),
    "eq": ("sbuf", [128, 512], CODE), "eqs": ("sbuf", [128, 512], U8),
    "aq": ("sbuf", [128, 256], CODE), "aqs": ("sbuf", [128, 256], U8),
    "k1": ("sbuf", [128, 256], CODE), "k1s": ("sbuf", [128, 256], U8),
    "k2": ("sbuf", [128, 512], CODE), "k2s": ("sbuf", [128, 512], U8),
    "r1": ("sbuf", [128, 256], CODE), "r1s": ("sbuf", [128, 256], U8),
    "r2": ("sbuf", [128, 256], CODE), "r2s": ("sbuf", [128, 256], U8),
    "hq": ("sbuf", [128, 512], CODE), "hqs": ("sbuf", [128, 512], U8),
    "w": ("sbuf", [128, 2560], F32),
    "gg": ("sbuf", [128, 2048], F32),
    "ht": ("sbuf", [128, 2048], BF),
    "yt": ("sbuf", [128, 1024], F32),
    "pu": ("psum", [128, 2560], F32),
    "py": ("psum", [128, 1536], F32),
}
SEMAPHORES = (["ld_w", "ld_v", "ld_a", "ld_s", "it1", "it2", "it3", "cv", "cvo", "eb", "eqd", "gov", "gos", "l1", "l2",
               "g1v", "g1s", "q1", "g2v", "g2s", "q2", "qa", "sa", "sb", "sc", "sl", "idn", "arr1", "arr2", "arrn",
               "sent", "stored"]
              + ["%s%d" % (n, b) for n in ("mb1_", "mb0_", "mb2_", "cb1_", "cb0_", "cb2_", "gv", "gs", "tr", "tt", "hc", "hp",
                                           "hq", "ym", "yc") for b in range(4)])
OTHER = {"v": "s", "s": "v"}


def rank_program(g, core, T, topo):
    rank = T.rank_of(core)
    if rank is None:
        return
    V, S, PE, SY = g.vector, g.scalar, g.tensor, g.sync
    sem = T.sem
    COPY = ActivationFunctionType.Copy
    chips = []
    for c in T.cores:
        if topo.chip(c) not in chips:
            chips.append(topo.chip(c))
    members = [[T.rank_of(c) for c in T.cores if topo.chip(c) == ch] for ch in chips]
    nch = len(chips)
    me = chips.index(topo.chip(core))
    par = members[me].index(rank)
    nbr = members[me][1 - par]

    def at(d):
        return members[(me + d) % nch]

    for q, lo in ((SY, 0), (S, 4)):
        for k in range(lo, lo + 4):
            q.dma_start(T.wl[16 * k:16 * k + 16, :], T.want[:, :]).then_inc(sem["ld_w"], 16)
    SY.dma_start(T.vt[:, :], T.v[:, :]).then_inc(sem["ld_v"], 16)
    for q, lo in ((SY, 0), (S, 4)):
        for k in range(lo, lo + 4):
            q.dma_start(T.sw[16 * k:16 * k + 16, :], T.slot[:, :]).then_inc(sem["ld_s"], 16)
    SY.dma_start(T.at[:, :], T.a[:, :]).then_inc(sem["ld_a"], 16)

    g.iota(T.e2[:, :], [[-128, 4]], 0, 4, allow_small_or_imprecise_dtypes=True).then_inc(sem["it2"], 1)
    g.iota(T.e1[:, :], [[1, 128], [-1, 4]], 0, 0, allow_small_or_imprecise_dtypes=True).then_inc(sem["it1"], 1)
    g.iota(T.e3[:, :], [[1, 128]], 0, -1, allow_small_or_imprecise_dtypes=True).then_inc(sem["it3"], 1)

    off_ranks = at(1) + at(2) + at(3) + at(4)
    off_eng = topo.engines(core, T.cores[off_ranks[0]])
    share = len(off_eng) // 4
    masks = [sum(1 << e for e in off_eng[share * m:share * m + share]) for m in range(4)]
    spare = [e for e in topo.engines(core, T.cores[nbr]) if e not in off_eng]
    masks.append(sum(1 << e for e in spare[::2][:share]))

    def send(items):
        trs = []
        for r, m, s, d, x in items:
            rid, pid, _ = topo.addr(T.cores[r])
            trs.append(RemoteDMATransfer(dst_ids=[DstId(rid=rid, pnc=pid)], dma_engine_mask=masks[m], remote_sem=sem[s],
                                         srcs=[x], dsts=[d], alu_op=0))
        g.remote_dma_fused(trs, local_sem=sem["sent"])

    g.wait_ge(sem["cv"], 1)
    send([(r, 2 * i + j, "l1", T.lst1[:, 8 * i + 4 * par:8 * i + 4 * par + 4], T.loff[:, 4 * r:4 * r + 4])
          for i, d in enumerate((-1, -2)) for j, r in enumerate(at(d))])
    send([(r, 2 * i + j, "l2", T.lst2[:, 8 * i + 4 * par:8 * i + 4 * par + 4], T.loff[:, 4 * r:4 * r + 4])
          for i, d in enumerate((-3, -4)) for j, r in enumerate(at(d))]
         + [(nbr, 4, "l2", T.lst2[:, 16:20], T.loff[:, 4 * nbr:4 * nbr + 4])])

    to1 = [(r, 2 * i + j, 128 * (1 - i) + 64 * par, 128 * i + 64 * j) for i, d in enumerate((1, 2)) for j, r in enumerate(at(d))]
    g.wait_ge(sem["q1"], 1)
    send([(r, m, "arr1", T.r1[:, d:d + 64].bitcast(dt.uint8), T.k1[:, x:x + 64].bitcast(dt.uint8)) for r, m, d, x in to1])
    send([(r, m, "arr1", T.r1s[:, d:d + 64], T.k1s[:, x:x + 64]) for r, m, d, x in to1])
    base = 64 + 64 * par
    own = 384 if par == 0 else 64
    pair = 384 if par == 0 else 0
    nland = 448 if par == 1 else 0
    to2 = [(r, 2 * i + j, 128 * (1 - i) + 64 * par, base + 128 * i + 64 * j) for i, d in enumerate((3, 4)) for j, r in enumerate(at(d))]
    g.wait_ge(sem["q2"], 1)
    send([(r, m, "arr2", T.r2[:, d:d + 64].bitcast(dt.uint8), T.k2[:, x:x + 64].bitcast(dt.uint8)) for r, m, d, x in to2]
         + [(nbr, 4, "arrn", T.k2[:, nland:nland + 64].bitcast(dt.uint8), T.k2[:, base + 256:base + 320].bitcast(dt.uint8))])
    send([(r, m, "arr2", T.r2s[:, d:d + 64], T.k2s[:, x:x + 64]) for r, m, d, x in to2]
         + [(nbr, 4, "arrn", T.k2s[:, nland:nland + 64], T.k2s[:, base + 256:base + 320])])
    g.wait_ge(sem["sent"], share * (4 + 5 + 4 + 4 + 5 + 5))

    def copy(q, out, in_, s):
        if q == "v":
            V.tensor_copy(out, in_).then_inc(sem[s], 1)
        else:
            S.activation(out, in_, COPY).then_inc(sem[s], 1)

    def wait(q, *pairs):
        for s, n in pairs:
            (V if q == "v" else S).wait_ge(sem[s], n)

    wait("v", ("ld_w", 128))
    V.tensor_scalar(T.loff[:, :], T.wl[:, :], 0, 4, AluOpType.max, AluOpType.mult).then_inc(sem["cv"], 1)
    V.tensor_scalar(T.lown[:, :], T.wl[:, 4 * rank:4 * rank + 4], 0, 4, AluOpType.max, AluOpType.mult).then_inc(sem["cvo"], 1)
    wait("v", ("it1", 1), ("it2", 1))
    for b in range(4):
        V.tensor_scalar(T.idt[:, 512 * b:512 * b + 512], T.e1[:, :], T.e2[:, b:b + 1], None, AluOpType.is_equal).then_inc(sem["eb"], 1)
    wait("v", ("eb", 4))
    V.quantize_mx(T.eq[:, :], T.eqs[:, :], T.idt[:, :]).then_inc(sem["eqd"], 1)

    goff = 0 if par == 0 else 64
    gown = 320 if par == 0 else 0
    for q, ts in (("v", (0, 1)), ("s", (2, 3))):
        wait(q, ("ld_v", 16), ("cvo", 1))
        for t in ts:
            copy(q, T.gt2[:, 4 * gown + t:4 * gown + 256:4], T.vt[:, t:2048].indirect(T.lown[:, 0:4]), "go" + q)
        wait(q, ("l1", 4 * share))
        for t in ts:
            copy(q, T.gt1[:, t:1024:4], T.vt[:, t:2048].indirect(T.lst1[:, 0:16]), "g1" + q)
        if q == "v":
            wait("v", ("g1v", 2), ("g1s", 2))
            V.quantize_mx(T.k1[:, :], T.k1s[:, :], T.gt1[:, :]).then_inc(sem["q1"], 1)
        wait(q, ("l2", 5 * share))
        for t in ts:
            copy(q, T.gt2[:, 4 * goff + t:4 * goff + 1280:4], T.vt[:, t:2048].indirect(T.lst2[:, 0:20]), "g2" + q)
    wait("v", ("gov", 2), ("gos", 2), ("g2v", 2), ("g2s", 2))
    V.quantize_mx(T.k2[:, 64:448], T.k2s[:, 64:448], T.gt2[:, :]).then_inc(sem["q2"], 1)

    wait("v", ("ld_a", 16))
    V.quantize_mx(T.aq[:, :], T.aqs[:, :], T.at[:, :]).then_inc(sem["qa"], 1)
    wait("v", ("ld_s", 128))
    V.tensor_scalar(T.s1i[:, :], T.sw[:, :], 128 * me, 640, AluOpType.is_lt, AluOpType.mult).then_inc(sem["sa"], 1)
    V.tensor_scalar(T.s2i[:, :], T.sw[:, :], 128 * me, None, AluOpType.subtract).then_inc(sem["sb"], 1)
    wait("v", ("it3", 1))
    V.tensor_scalar(T.idn[:, :], T.e3[:, :], 0.0, None, AluOpType.is_equal).then_inc(sem["idn"], 1)
    wait("v", ("sa", 1), ("sb", 1))
    V.tensor_tensor(T.s3i[:, :], T.s1i[:, :], T.s2i[:, :], AluOpType.add).then_inc(sem["sc"], 1)
    wait("v", ("sc", 1))
    V.tensor_copy(T.sl[:, :], T.s3i[:, :]).then_inc(sem["sl"], 1)

    bank0, bank2, bankt = (4, 0, 1, 2), (3, 4, 0, 1), (2, 3, 4)

    def P(k, n):
        return T.pu[:, 512 * k:512 * k + n]

    def E(b):
        return T.eq[:, 128 * b:128 * b + 128], T.eqs[:, 128 * b:128 * b + 128]

    PE.wait_ge(sem["eqd"], 1)
    PE.wait_ge(sem["arr1"], 8 * share)
    for b in range(4):
        PE.matmul_mx(P(b, 256), *E(b), T.r1[:, :], T.r1s[:, :], True, True).then_inc(sem["mb1_%d" % b], 1)
    PE.wait_ge(sem["q2"], 1)
    PE.wait_ge(sem["arrn"], 2 * share)
    for b in range(4):
        if b:
            PE.wait_ge(sem["cb1_%d" % (b - 1)], 1)
        PE.matmul_mx(P(bank0[b], 128), *E(b), T.k2[:, pair:pair + 128], T.k2s[:, pair:pair + 128], True, True).then_inc(sem["mb0_%d" % b], 1)
    PE.wait_ge(sem["arr2"], 8 * share)
    for b in range(4):
        PE.wait_ge(sem["cb1_3"] if b == 0 else sem["cb0_%d" % (b - 1)], 1)
        PE.matmul_mx(P(bank2[b], 256), *E(b), T.r2[:, :], T.r2s[:, :], True, True).then_inc(sem["mb2_%d" % b], 1)
    PE.wait_ge(sem["idn"], 1)
    PE.wait_ge(sem["qa"], 1)

    def product(o, k):
        PE.wait_ge(sem["hq%d" % o], 1)
        PE.matmul_mx(T.py[:, 512 * k:512 * k + 256], T.hq[:, 128 * o:128 * o + 128], T.hqs[:, 128 * o:128 * o + 128],
                     T.aq[:, :], T.aqs[:, :], True, True).then_inc(sem["ym%d" % o], 1)

    for o in range(3):
        PE.wait_ge(sem["gv%d" % o], 1)
        PE.wait_ge(sem["gs%d" % o], 1)
        PE.wait_ge(sem["cb0_3"] if o == 0 else sem["cb2_%d" % (o - 1)], 1)
        for t in range(4):
            PE.transpose(T.pu[:, 512 * bankt[o] + t:512 * bankt[o] + 512:4], T.gg[:, 512 * o + t:512 * o + 512:4], T.idn[:, :]).then_inc(sem["tr%d" % o], 1)
    PE.wait_ge(sem["gv3"], 1)
    PE.wait_ge(sem["gs3"], 1)
    for t in range(4):
        PE.wait_ge(sem[("cb2_2", "cb2_3", "hc0", "hc1")[t]], 1)
        PE.transpose(P(t, 128), T.gg[:, 1536 + t:2048:4], T.idn[:, :]).then_inc(sem["tt%d" % t], 1)
        if t == 1:
            product(0, 0)
    product(1, 1)
    product(2, 2)
    PE.wait_ge(sem["yc0"], 1)
    product(3, 0)

    def towin(q, b):
        for n, banks, first, width in (("b1_", (0, 1, 2, 3), 384, 256), ("b0_", bank0, 0, 128)):
            pass

    def unpacked(q, n, b, bank, first, width):
        wait(q, ("m%s%d" % (n, b), 1))
        copy(q, T.w[:, 640 * b + first:640 * b + first + width], P(bank, width), "c%s%d" % (n, b))

    def choose(q, o):
        wait(q, ("sl", 1), ("cb1_%d" % o, 1), ("cb0_%d" % o, 1), ("cb2_%d" % o, 1))
        k = 0 if q == "v" else 1
        copy(q, T.gg[:, 512 * o + 256 * k:512 * o + 256 * k + 256], T.w[:, 640 * o:640 * o + 640].indirect(T.sl[:, 16 * k:16 * k + 16]), "g%s%d" % (q, o))

    def block(q, o):
        wait(q, ("tr%d" % o, 4))
        copy(q, T.ht[:, 512 * o:512 * o + 512], P(bankt[o], 512), "hc%d" % o)

    def piece(q, t):
        wait(q, ("tt%d" % t, 1))
        copy(q, T.ht[:, 1536 + t:2048:4], P(t, 128), "hp%d" % t)

    def quant(o):
        wait("v", *([("hc%d" % o, 1)] if o < 3 else [("hp%d" % t, 1) for t in range(4)]))
        V.quantize_mx(T.hq[:, 128 * o:128 * o + 128], T.hqs[:, 128 * o:128 * o + 128], T.ht[:, 512 * o:512 * o + 512]).then_inc(sem["hq%d" % o], 1)

    def result(q, o, k):
        wait(q, ("ym%d" % o, 1))
        copy(q, T.yt[:, 256 * o:256 * o + 256], T.py[:, 512 * k:512 * k + 256], "yc%d" % o)

    for q, bs in (("v", (0, 2)), ("s", (1, 3))):
        for b in bs:
            unpacked(q, "b1_", b, b, 384, 256)
        for b in bs:
            unpacked(q, "b0_", b, bank0[b], 0, 128)
        for o, b in ((0, bs[0]), (1, bs[1])):
            unpacked(q, "b2_", b, bank2[b], 128, 256)
            choose(q, o)
        choose(q, 2)
        choose(q, 3)
    block("v", 1)
    block("s", 0)
    quant(0)
    quant(1)
    block("s", 2)
    quant(2)
    piece("s", 0)
    result("s", 0, 0)
    piece("s", 2)
    piece("v", 1)
    piece("v", 3)
    quant(3)
    result("v", 1, 1)
    result("s", 2, 2)
    result("v", 3, 0)

    def store_h(o):
        for s in (["hc%d" % o] if o < 3 else ["hp%d" % t for t in range(4)]):
            SY.wait_ge(sem[s], 1)
        SY.dma_start(T.h[:, 512 * o:512 * o + 512], T.ht[:, 512 * o:512 * o + 512]).then_inc(sem["stored"], 16)

    def store_y(o):
        SY.wait_ge(sem["yc%d" % o], 1)
        SY.dma_start(T.y[:, 256 * o:256 * o + 256], T.yt[:, 256 * o:256 * o + 256]).then_inc(sem["stored"], 16)

    store_h(0)
    store_h(1)
    store_h(2)
    store_y(0)
    store_h(3)
    for o in (1, 2, 3):
        store_y(o)
    SY.wait_ge(sem["stored"], 128)
